import numpy as np, ml_dtypes
CORES = [16,32,48,64,80]
N = 5
import mx_ref
NC, G = 128, 2
C, C2 = np.float32(0.041), np.float32(0.01834)
BF = ml_dtypes.bfloat16
def cut(t, i, w=512):
    return t[:, w * i:w * i + w]
def tile(rs):
    return np.stack(rs, axis=2).reshape(128, -1).astype(BF)
def layer(w, X):
    out = []
    for i in range(G):
        for t in range(len(X)):
            p = mx_ref.matmul(mx_ref.quantize(cut(w, len(X) * i + t)), X[t])
            z = p if t == 0 else z + p
        out.append(z)
    return out
def act(Z):
    return [np.maximum(s * z, 0) * C for z in Z for s in (1, -1)]
def act2(Z):
    return [np.maximum(s * z, 0) * C2 for z in Z for s in (1, -1)]
def setup_inputs(rng):
    def f(*shape):
        return mx_ref.flush((rng.standard_normal(shape, dtype=np.float32) * np.exp2(rng.integers(-2, 3, shape[:-1] + (1,)))).astype(BF))
    return {"x": f(N, 128, 4 * NC), "w1": f(N, 128, G * 512), "w2": f(N, 128, G * 512), "w3": f(N, 128, G * 512), "w4": f(N, 128, 512)}
def setup_inputs_blocks(rng):
    d = setup_inputs(rng)
    for k in ("x", "w1", "w2", "w3", "w4"): d[k] = mx_ref.spread(d[k], rng, 2)
    return d
def setup_inputs_wide(rng):
    d = setup_inputs(rng)
    for k in ("x", "w1", "w2", "w3", "w4"): d[k] = mx_ref.flush((d[k].astype(np.float32) * np.exp2(rng.integers(-4, 5, (N, 1, 1))).astype(np.float32)).astype(BF))
    return d
def reference(x, w1, w2, w3, w4, own=None):
    X = [mx_ref.quantize(x[j]) for j in range(N)]
    t = np.stack([np.stack([tile(act(layer(w1[r], [X[c]]))) for c in range(N)]) for r in range(N)])
    uset = t if own is None else own["t"]
    h = np.zeros((N, 128, 4 * NC), BF)
    for c in range(N):
        for r in range(N):
            P = layer(w2[r], [mx_ref.quantize(uset[r][c])])
            Z = P if r == 0 else [z + p for z, p in zip(Z, P)]
        h[c] = tile(act2(Z))
    use = h if own is None else own["h"]
    H = [mx_ref.quantize(use[j]) for j in range(N)]
    y = np.zeros((N, 128, NC), np.float32)
    for c in range(N):
        for r in range(N):
            p = mx_ref.matmul(mx_ref.quantize(w4[r]), mx_ref.quantize(tile(act(layer(w3[r], [H[c]])))))
            y[c] = p if r == 0 else y[c] + p
    return {"t": t, "h": h, "y": y}

@@ -1,0 +1,336 @@
+import numpy as np
+from concourse.bass import DstId, RemoteDMATransfer
+from concourse.mybir import dt, AluOpType, ActivationFunctionType
+
+N = 5
+SIM_CORES = 96
+C1 = float(np.float32(0.041))
+C2 = float(np.float32(0.01834))
+FW = 160
+WC = 384
+
+CODES = "float8_e4m3fn_x4"
+SCRATCH = {
+    "xin": ("sbuf", [128, 512], "bfloat16"),
+    "w1in": ("sbuf", [128, 1024], "bfloat16"),
+    "w2in": ("sbuf", [128, 1024], "bfloat16"),
+    "w3in": ("sbuf", [128, 1024], "bfloat16"),
+    "w4in": ("sbuf", [128, 512], "bfloat16"),
+    "xq": ("sbuf", [128, N * 128], CODES),
+    "xs": ("sbuf", [128, N * 128], "uint8"),
+    "w1q": ("sbuf", [128, 256], CODES),
+    "w1s": ("sbuf", [128, 256], "uint8"),
+    "w2q": ("sbuf", [128, 256], CODES),
+    "w2s": ("sbuf", [128, 256], "uint8"),
+    "wq": ("sbuf", [128, N * WC], CODES),
+    "ws": ("sbuf", [128, N * WC], "uint8"),
+    "tt": ("sbuf", [128, N * 512], "bfloat16"),
+    "tq": ("sbuf", [128, N * 128], CODES),
+    "ts": ("sbuf", [128, N * 128], "uint8"),
+    "hh": ("sbuf", [128, 512], "bfloat16"),
+    "hq": ("sbuf", [128, 128], CODES),
+    "hs": ("sbuf", [128, 128], "uint8"),
+    "uu": ("sbuf", [128, N * 512], "bfloat16"),
+    "uq": ("sbuf", [128, N * 128], CODES),
+    "us": ("sbuf", [128, N * 128], "uint8"),
+    "pp": ("sbuf", [128, N * 256], "float32"),
+    "ld": ("sbuf", [128, 256], "float32"),
+    "lc": ("sbuf", [128, 256 - FW], "float32"),
+    "lf": ("sbuf", [128, 256], "float32"),
+    "al": ("sbuf", [128, 768], "float32"),
+    "asum": ("sbuf", [128, 256], "float32"),
+    "yo": ("sbuf", [128, 128], "float32"),
+    "ps": ("psum", [128, 4096], "float32"),
+}
+_ONE = ["ld_x", "ld_w1", "ld_w2", "ld_w3", "ld_w4", "q_x", "q_w1", "q_w2", "q_w34", "c1", "c2", "c3", "hA", "hB", "tlh", "qh",
+        "yd", "yev", "st", "bsent", "psent", "da", "dc", "fa1", "fa2", "ha1", "ha2", "ha3", "hb", "hf1", "hf2", "wr"]
+_FIVE = ["z0_", "z1_", "tl_", "qt_", "s0_", "s1_", "ev_", "v0_", "v1_", "tu_", "qu_", "xa_", "wa_"]
+SEMAPHORES = _ONE + [n + str(k) for n in _FIVE for k in range(N)]
+
+
+def _bits(mask):
+    return [b for b in range(mask.bit_length()) if (mask >> b) & 1]
+
+
+def _mask(bits):
+    m = 0
+    for b in bits:
+        m |= 1 << b
+    return m
+
+
+def _crew(c, topo):
+    chip = [k for k in range(SIM_CORES) if k != c and topo.chip(k) == topo.chip(c)]
+    near = [k for k in chip if topo.die(k) == topo.die(c)]
+    far = [k for k in chip if topo.die(k) != topo.die(c)]
+    return near[0], far[0], far[1], far[2]
+
+
+def _onchip(c, near, far, topo):
+    return _bits(topo.mask(c, near) & ~topo.mask(c, far))
+
+
+def _dst(c, topo):
+    rid, pid, _ = topo.addr(c)
+    return DstId(rid=rid, pnc=pid)
+
+
+def _send(g, topo, dst, out, in_, sem, lsem, mask):
+    rid, pid, _ = topo.addr(dst)
+    g.remote_dma(out_ap=out, in_ap=in_, remote_sem=sem, local_sem=lsem, pid=pid, routing_id=rid, dma_engine_mask=mask)
+
+
+def _spread(g, topo, dsts, view, sem, lsem, mask):
+    g.remote_dma_fused([RemoteDMATransfer(dst_ids=[_dst(p, topo) for p in dsts], dma_engine_mask=mask, remote_sem=sem,
+                                          srcs=[view], dsts=[view for p in dsts])], local_sem=lsem)
+
+
+def rank_program(g, core, T, topo):
+    rank = T.rank_of(core)
+    if rank is not None:
+        _rank(g, core, rank, T, topo)
+        return
+    for s in range(N):
+        adder, ra, rb, rp = _crew(T.cores[s], topo)
+        if core == adder:
+            _adder(g, core, s, T, topo)
+        elif core in (ra, rb, rp):
+            _relay(g, core, s, (ra, rb, rp).index(core), T, topo)
+
+
+def _relay(g, core, s, part, T, topo):
+    S = T.sem
+    peers = [T.cores[(s + k) % N] for k in range(1, N)]
+    mask = topo.mask(core, peers[0])
+    n = len(_bits(mask))
+    came = len(_onchip(T.cores[s], core, peers[0], topo))
+    if part == 2:
+        g.wait_ge(S.wr, came)
+        _spread(g, topo, peers, T.ws[:, WC * s:WC * s + WC], S["wa_%d" % s], S.bsent, mask)
+        g.wait_ge(S.bsent, n)
+        return
+    a = WC * s + part * (WC // 2)
+    v = T.wq[:, a:a + WC // 2].bitcast(dt.uint8)
+    g.wait_ge(S.wr, came // 2)
+    for p in peers:
+        _send(g, topo, p, v, v, S["wa_%d" % s], S.bsent, mask)
+    g.wait_ge(S.bsent, n * len(peers))
+
+
+def _adder(g, core, s, T, topo):
+    S, v = T.sem, g.vector
+    owner, far = T.cores[s], T.cores[(s + 1) % N]
+    mask = topo.mask(core, far) & topo.mask(core, owner)
+    n = len(_bits(mask))
+    came = len(_bits(topo.mask(far, core)))
+    v.wait_ge(S.ha1, came)
+    v.wait_ge(S.ha2, came)
+    v.tensor_tensor(T.asum[:, FW:256], T.al[:, FW:256], T.al[:, 256 + FW:512], AluOpType.add).then_inc(S.hf1, 1)
+    v.tensor_tensor(T.asum[:, 0:FW], T.al[:, 0:FW], T.al[:, 256:256 + FW], AluOpType.add).then_inc(S.hb, 1)
+    v.wait_ge(S.hb, 1)
+    v.wait_ge(S.ha3, came)
+    v.tensor_tensor(T.asum[:, 0:FW], T.asum[:, 0:FW], T.al[:, 512:512 + FW], AluOpType.add).then_inc(S.hf2, 1)
+    g.wait_ge(S.hf1, 1)
+    _send(g, topo, owner, T.lf[:, FW:256], T.asum[:, FW:256], S.fa1, S.bsent, mask)
+    g.wait_ge(S.hf2, 1)
+    _send(g, topo, owner, T.lf[:, 0:FW], T.asum[:, 0:FW], S.fa2, S.bsent, mask)
+    g.wait_ge(S.bsent, 2 * n)
+
+
+def _rank(g, core, r, T, topo):
+    S, v, sc, te, sy = T.sem, g.vector, g.scalar, g.tensor, g.sync
+    Relu, Copy = ActivationFunctionType.Relu, ActivationFunctionType.Copy
+    add, mx, mul = AluOpType.add, AluOpType.max, AluOpType.mult
+    peers = [T.cores[(r + k) % N] for k in range(1, N)]
+    _, ra, rb, rp = _crew(core, topo)
+    off = topo.mask(core, peers[0])
+    rest = _onchip(core, ra, peers[0], topo)
+    who = [(r - k) % N for k in range(N)]
+    n = len(_bits(off))
+
+    sy.dma_start(T.xin[:], T.x[:]).then_inc(S.ld_x, 16)
+    sy.dma_start(T.w1in[:], T.w1[:]).then_inc(S.ld_w1, 16)
+    sy.dma_start(T.w3in[:], T.w3[:]).then_inc(S.ld_w3, 16)
+    sy.dma_start(T.w4in[:], T.w4[:]).then_inc(S.ld_w4, 16)
+    sy.dma_start(T.w2in[:], T.w2[:]).then_inc(S.ld_w2, 16)
+    sy.wait_ge(S.psent, N * n)
+    for k in range(N):
+        sy.wait_ge(S["tl_%d" % k], 4)
+        sy.dma_start(T.t[who[k]], T.tt[:, 512 * k:512 * k + 512]).then_inc(S.st, 16)
+    sy.wait_ge(S.tlh, 4)
+    sy.dma_start(T.h[:], T.hh[:]).then_inc(S.st, 16)
+    sy.wait_ge(S.yev, 1)
+    sy.dma_start(T.y[:], T.yo[:]).then_inc(S.st, 16)
+    sy.wait_ge(S.st, 16 * (N + 2))
+
+    xs = T.xs[:, 128 * r:128 * r + 128]
+    xq = T.xq[:, 128 * r:128 * r + 128].bitcast(dt.uint8)
+    g.wait_ge(S.q_x, 1)
+    _spread(g, topo, peers, xs, S["xa_%d" % r], S.bsent, off)
+    _spread(g, topo, peers[:2], xq, S["xa_%d" % r], S.bsent, off)
+    _spread(g, topo, peers[2:], xq, S["xa_%d" % r], S.bsent, off)
+    g.wait_ge(S.q_w34, 2)
+    half = len(rest) // 2
+    parts = []
+    for i, p in enumerate((ra, rb)):
+        a = WC * r + i * (WC // 2)
+        view = T.wq[:, a:a + WC // 2].bitcast(dt.uint8)
+        parts.append(RemoteDMATransfer(dst_ids=[_dst(p, topo)], dma_engine_mask=_mask(rest[half * i:half * i + half]),
+                                       remote_sem=S.wr, srcs=[view], dsts=[view]))
+    g.remote_dma_fused(parts, local_sem=S.bsent)
+    ws = T.ws[:, WC * r:WC * r + WC]
+    _send(g, topo, rp, ws, ws, S.wr, S.bsent, _mask(rest))
+    for k in range(1, N):
+        owner = T.cores[who[k]]
+        adder = _crew(owner, topo)[0]
+        p = 256 * k
+        g.wait_ge(S["ev_%d" % k], 2)
+        if k < 3:
+            _send(g, topo, adder, T.al[:, 256 * (k - 1):256 * k], T.pp[:, p:p + 256], S["ha%d" % k], S.psent, off)
+        elif k == 3:
+            _send(g, topo, adder, T.al[:, 512:512 + FW], T.pp[:, p:p + FW], S.ha3, S.psent, off)
+            _send(g, topo, owner, T.lc[:], T.pp[:, p + FW:p + 256], S.dc, S.psent, off)
+        else:
+            _send(g, topo, owner, T.ld[:], T.pp[:, p:p + 256], S.da, S.psent, off)
+    g.wait_ge(S.bsent, 3 * n + 2 * len(rest))
+
+    def bank(b):
+        return T.ps[:, 512 * b:512 * b + 128]
+
+    def act_v(buf, o, b, src, c, sem):
+        v.tensor_scalar(buf[:, o + b:o + 512:4], src, 0.0, c, op0=mx, op1=mul).then_inc(sem, 1)
+        v.tensor_scalar(buf[:, o + b + 1:o + 512:4], src, -c, 0.0, op0=mul, op1=mx).then_inc(sem, 1)
+
+    def act_s(buf, o, b, src, c, sem):
+        sc.activation(buf[:, o + b:o + 512:4], src, Relu, scale=c).then_inc(sem, 1)
+        sc.activation(buf[:, o + b + 1:o + 512:4], src, Relu, scale=-c).then_inc(sem, 1)
+
+    def zb(k): return 2 * (k % 2)
+    def sb(k): return 4 + 2 * (k % 2)
+    def vb(k): return 2 * (k % 3)
+    YB = 6
+
+    def t_z(k):
+        s = who[k]
+        if k:
+            te.wait_ge(S["xa_%d" % s], 2 * n)
+        else:
+            te.wait_ge(S.q_x, 1)
+            te.wait_ge(S.q_w1, 1)
+        for i in range(2):
+            te.matmul_mx(bank(zb(k) + i), T.w1q[:, 128 * i:128 * i + 128], T.w1s[:, 128 * i:128 * i + 128],
+                         T.xq[:, 128 * s:128 * s + 128], T.xs[:, 128 * s:128 * s + 128], True, True
+                         ).then_inc(S["z%d_%d" % (i, k)], 1)
+
+    def t_s(k):
+        if k == 0:
+            te.wait_ge(S.q_w2, 1)
+        if k >= 2:
+            te.wait_ge(S["ev_%d" % (k - 2)], 2)
+        te.wait_ge(S["qt_%d" % k], 1)
+        for i in range(2):
+            te.matmul_mx(bank(sb(k) + i), T.w2q[:, 128 * i:128 * i + 128], T.w2s[:, 128 * i:128 * i + 128],
+                         T.tq[:, 128 * k:128 * k + 128], T.ts[:, 128 * k:128 * k + 128], True, True
+                         ).then_inc(S["s%d_%d" % (i, k)], 1)
+
+    def t_v(k):
+        s = who[k]
+        if k:
+            te.wait_ge(S["wa_%d" % s], 3 * n)
+        else:
+            te.wait_ge(S.q_w34, 2)
+            te.wait_ge(S.ev_3, 2)
+            te.wait_ge(S.ev_4, 2)
+            te.wait_ge(S.qh, 1)
+        for i in range(2):
+            a = WC * s + 128 * i
+            te.matmul_mx(bank(vb(k) + i), T.wq[:, a:a + 128], T.ws[:, a:a + 128], T.hq[:], T.hs[:], True, True
+                         ).then_inc(S["v%d_%d" % (i, k)], 1)
+
+    def t_y(k):
+        a = WC * who[k] + 256
+        te.wait_ge(S["qu_%d" % k], 1)
+        m = te.matmul_mx(bank(YB), T.wq[:, a:a + 128], T.ws[:, a:a + 128], T.uq[:, 128 * k:128 * k + 128],
+                         T.us[:, 128 * k:128 * k + 128], k == 0, k == N - 1)
+        if k == N - 1:
+            m.then_inc(S.yd, 1)
+
+    t_z(0); t_s(0)
+    t_z(1); t_z(2); t_s(1); t_z(3); t_s(2); t_z(4); t_s(3); t_s(4)
+    t_v(0); t_v(1); t_v(2); t_y(0); t_v(3); t_y(1); t_v(4); t_y(2); t_y(3); t_y(4)
+
+    def v_r(k):
+        v.wait_ge(S["z0_%d" % k], 1)
+        act_v(T.tt, 512 * k, 0, bank(zb(k)), C1, S["tl_%d" % k])
+
+    def v_q(k):
+        v.wait_ge(S["tl_%d" % k], 4)
+        v.quantize_mx(T.tq[:, 128 * k:128 * k + 128], T.ts[:, 128 * k:128 * k + 128], T.tt[:, 512 * k:512 * k + 512]
+                      ).then_inc(S["qt_%d" % k], 1)
+
+    def v_e(k):
+        v.wait_ge(S["s0_%d" % k], 1)
+        v.tensor_copy(T.pp[:, 256 * k:256 * k + 128], bank(sb(k))).then_inc(S["ev_%d" % k], 1)
+
+    def v_ru(k):
+        v.wait_ge(S["v0_%d" % k], 1)
+        act_v(T.uu, 512 * k, 0, bank(vb(k)), C1, S["tu_%d" % k])
+
+    def v_qu(k):
+        v.wait_ge(S["tu_%d" % k], 4)
+        v.quantize_mx(T.uq[:, 128 * k:128 * k + 128], T.us[:, 128 * k:128 * k + 128], T.uu[:, 512 * k:512 * k + 512]
+                      ).then_inc(S["qu_%d" % k], 1)
+
+    v.wait_ge(S.ld_x, 16)
+    v.quantize_mx(T.xq[:, 128 * r:128 * r + 128], T.xs[:, 128 * r:128 * r + 128], T.xin[:]).then_inc(S.q_x, 1)
+    v.wait_ge(S.ld_w1, 16)
+    v.quantize_mx(T.w1q[:], T.w1s[:], T.w1in[:]).then_inc(S.q_w1, 1)
+    v.wait_ge(S.ld_w3, 16)
+    v.quantize_mx(T.wq[:, WC * r:WC * r + 256], T.ws[:, WC * r:WC * r + 256], T.w3in[:]).then_inc(S.q_w34, 1)
+    v.wait_ge(S.ld_w4, 16)
+    v.quantize_mx(T.wq[:, WC * r + 256:WC * r + 384], T.ws[:, WC * r + 256:WC * r + 384], T.w4in[:]).then_inc(S.q_w34, 1)
+    v_r(0); v_q(0)
+    v.wait_ge(S.ld_w2, 16)
+    v.quantize_mx(T.w2q[:], T.w2s[:], T.w2in[:]).then_inc(S.q_w2, 1)
+    v_e(0)
+    v_r(1); v_q(1); v_r(2); v_e(1); v_q(2); v_r(3); v_e(2); v_q(3); v_r(4); v_e(3); v_q(4); v_e(4)
+
+    def acc(a, b, src, sem):
+        v.tensor_tensor(T.pp[:, a:b], T.pp[:, a:b], src, add).then_inc(sem, 1)
+
+    v.wait_ge(S.ev_0, 2)
+    v.wait_ge(S.fa1, n)
+    acc(FW, 256, T.lf[:, FW:256], S.c1)
+    v.wait_ge(S.c1, 1)
+    v.wait_ge(S.dc, n)
+    acc(FW, 256, T.lc[:], S.c2)
+    v.wait_ge(S.c2, 1)
+    v.wait_ge(S.da, n)
+    acc(0, 256, T.ld[:], S.c3)
+    v.wait_ge(S.c3, 1)
+    v.wait_ge(S.fa2, n)
+    acc(0, 128, T.lf[:, 0:128], S.hA)
+    acc(128, FW, T.lf[:, 128:FW], S.hB)
+    v.wait_ge(S.hB, 1)
+    act_v(T.hh, 0, 2, T.pp[:, 128:256], C2, S.tlh)
+    v.wait_ge(S.tlh, 4)
+    v.quantize_mx(T.hq[:], T.hs[:], T.hh[:]).then_inc(S.qh, 1)
+    v_ru(0); v_ru(1); v_qu(0); v_ru(2); v_qu(1); v_ru(3); v_qu(2); v_ru(4); v_qu(3); v_qu(4)
+    v.wait_ge(S.yd, 1)
+    v.tensor_copy(T.yo[:], bank(YB)).then_inc(S.yev, 1)
+
+    def s_r(k):
+        sc.wait_ge(S["z1_%d" % k], 1)
+        act_s(T.tt, 512 * k, 2, bank(zb(k) + 1), C1, S["tl_%d" % k])
+
+    def s_e(k):
+        sc.wait_ge(S["s1_%d" % k], 1)
+        sc.activation(T.pp[:, 256 * k + 128:256 * k + 256], bank(sb(k) + 1), Copy).then_inc(S["ev_%d" % k], 1)
+
+    s_r(0); s_e(0)
+    s_r(1); s_r(2); s_e(1); s_r(3); s_e(2); s_r(4); s_e(3); s_e(4)
+    sc.wait_ge(S.hA, 1)
+    act_s(T.hh, 0, 0, T.pp[:, 0:128], C2, S.tlh)
+    for k in range(N):
+        sc.wait_ge(S["v1_%d" % k], 1)
+        act_s(T.uu, 512 * k, 2, bank(vb(k) + 1), C1, S["tu_%d" % k])

@@ -8,6 +8,8 @@ C1 = float(np.float32(0.041))
 C2 = float(np.float32(0.01834))
 FW = 160
 WC = 384
+ND = 3
+BYS = (1, 3)
 
 CODES = "float8_e4m3fn_x4"
 SCRATCH = {
@@ -36,15 +38,17 @@ SCRATCH = {
     "pp": ("sbuf", [128, N * 256], "float32"),
     "ld": ("sbuf", [128, 256], "float32"),
     "lc": ("sbuf", [128, 256 - FW], "float32"),
+    "pb": ("sbuf", [128, 256 - FW], "float32"),
     "lf": ("sbuf", [128, 256], "float32"),
     "al": ("sbuf", [128, 768], "float32"),
     "asum": ("sbuf", [128, 256], "float32"),
     "yo": ("sbuf", [128, 128], "float32"),
     "ps": ("psum", [128, 4096], "float32"),
 }
-_ONE = ["ld_x", "ld_w1", "ld_w2", "ld_w3", "ld_w4", "q_x", "q_w1", "q_w2", "q_w34", "c1", "c2", "c3", "hA", "hB", "tlh", "qh",
-        "yd", "yev", "st", "bsent", "psent", "da", "dc", "fa1", "fa2", "ha1", "ha2", "ha3", "hb", "hf1", "hf2", "wr"]
-_FIVE = ["z0_", "z1_", "tl_", "qt_", "s0_", "s1_", "ev_", "v0_", "v1_", "tu_", "qu_", "xa_", "wa_"]
+_ONE = ["ld_x", "ld_w1", "ld_w2", "ld_w3", "ld_w4", "q_x", "q_w1", "q_w2", "q_w3", "q_w4", "c1", "c2", "hA", "hB", "tlh", "qh",
+        "yd", "yev", "st", "bsent", "psent", "fsent", "da", "dc", "fa1", "fa2", "ha1", "ha2", "ha3", "hb", "hf1", "hf2",
+        "wr", "wb", "wc", "xr", "pr"]
+_FIVE = ["z0_", "z1_", "tl_", "qt_", "s0_", "s1_", "ev_", "v0_", "v1_", "vh_", "tu_", "qu_", "xa_", "wa_", "wb_"]
 SEMAPHORES = _ONE + [n + str(k) for n in _FIVE for k in range(N)]
 
 
@@ -59,11 +63,22 @@ def _mask(bits):
     return m
 
 
+def _count(src, dst, topo):
+    return len(_bits(topo.mask(src, dst)))
+
+
 def _crew(c, topo):
-    chip = [k for k in range(SIM_CORES) if k != c and topo.chip(k) == topo.chip(c)]
+    mate = [k for k in range(SIM_CORES) if topo.mates(topo.chip(k), topo.chip(c))]
+    chip = sorted((k for k in range(SIM_CORES) if k != c and topo.chip(k) == topo.chip(c)),
+                  key=lambda k: topo.may_write(k, mate[0]))
     near = [k for k in chip if topo.die(k) == topo.die(c)]
     far = [k for k in chip if topo.die(k) != topo.die(c)]
-    return near[0], far[0], far[1], far[2]
+    return {"adder": near[0], "passer": near[1], "wb": near[2], "wa": far[0], "wp": far[1], "wc": far[-1],
+            "fw": [k for k in mate if topo.may_write(k, c)]}
+
+
+def _forwarder(d, s, T, topo):
+    return _crew(T.cores[d], topo)["fw"][(d - s) % N - 1]
 
 
 def _onchip(c, near, far, topo):
@@ -85,44 +100,53 @@ def _spread(g, topo, dsts, view, sem, lsem, mask):
                                           srcs=[view], dsts=[view for p in dsts])], local_sem=lsem)
 
 
+def _wview(T, s, part):
+    if part == "p":
+        return T.ws[:, WC * s:WC * s + WC]
+    a = WC * s + 128 * "abc".index(part)
+    return T.wq[:, a:a + 128].bitcast(dt.uint8)
+
+
 def rank_program(g, core, T, topo):
     rank = T.rank_of(core)
     if rank is not None:
         _rank(g, core, rank, T, topo)
         return
     for s in range(N):
-        adder, ra, rb, rp = _crew(T.cores[s], topo)
-        if core == adder:
+        crew = _crew(T.cores[s], topo)
+        if core == crew["adder"]:
             _adder(g, core, s, T, topo)
-        elif core in (ra, rb, rp):
-            _relay(g, core, s, (ra, rb, rp).index(core), T, topo)
+        elif core == crew["passer"]:
+            _passer(g, core, s, T, topo)
+        elif core in (crew["wa"], crew["wb"], crew["wc"], crew["wp"]):
+            _weights(g, core, s, crew, T, topo)
+        elif core in crew["fw"]:
+            _forward(g, core, s, T, topo)
 
 
-def _relay(g, core, s, part, T, topo):
+def _relay_x(g, core, s, view, T, topo):
     S = T.sem
-    peers = [T.cores[(s + k) % N] for k in range(1, N)]
+    peers = [T.cores[(s + k) % N] for k in range(1 + ND, N)]
     mask = topo.mask(core, peers[0])
-    n = len(_bits(mask))
-    came = len(_onchip(T.cores[s], core, peers[0], topo))
-    if part == 2:
-        g.wait_ge(S.wr, came)
-        _spread(g, topo, peers, T.ws[:, WC * s:WC * s + WC], S["wa_%d" % s], S.bsent, mask)
-        g.wait_ge(S.bsent, n)
-        return
-    a = WC * s + part * (WC // 2)
-    v = T.wq[:, a:a + WC // 2].bitcast(dt.uint8)
-    g.wait_ge(S.wr, came // 2)
-    for p in peers:
-        _send(g, topo, p, v, v, S["wa_%d" % s], S.bsent, mask)
-    g.wait_ge(S.bsent, n * len(peers))
+    g.wait_ge(S.xr, len(_onchip(T.cores[s], core, peers[0], topo)))
+    _spread(g, topo, peers, view, S["xa_%d" % s], S.bsent, mask)
+    return mask
+
+
+def _passer(g, core, s, T, topo):
+    S = T.sem
+    mask = _relay_x(g, core, s, T.xq[:, 128 * s:128 * s + 128].bitcast(dt.uint8), T, topo)
+    owner = T.cores[(s - 3) % N]
+    g.wait_ge(S.pr, len(_onchip(T.cores[s], core, owner, topo)))
+    _send(g, topo, owner, T.lc[:], T.pb[:], S.dc, S.bsent, mask)
+    g.wait_ge(S.bsent, 2 * len(_bits(mask)))
 
 
 def _adder(g, core, s, T, topo):
     S, v = T.sem, g.vector
     owner, far = T.cores[s], T.cores[(s + 1) % N]
-    mask = topo.mask(core, far) & topo.mask(core, owner)
-    n = len(_bits(mask))
-    came = len(_bits(topo.mask(far, core)))
+    mask = topo.mask(core, owner)
+    came = _count(far, core, topo)
     v.wait_ge(S.ha1, came)
     v.wait_ge(S.ha2, came)
     v.tensor_tensor(T.asum[:, FW:256], T.al[:, FW:256], T.al[:, 256 + FW:512], AluOpType.add).then_inc(S.hf1, 1)
@@ -130,11 +154,44 @@ def _adder(g, core, s, T, topo):
     v.wait_ge(S.hb, 1)
     v.wait_ge(S.ha3, came)
     v.tensor_tensor(T.asum[:, 0:FW], T.asum[:, 0:FW], T.al[:, 512:512 + FW], AluOpType.add).then_inc(S.hf2, 1)
+    xmask = _relay_x(g, core, s, T.xs[:, 128 * s:128 * s + 128], T, topo)
     g.wait_ge(S.hf1, 1)
-    _send(g, topo, owner, T.lf[:, FW:256], T.asum[:, FW:256], S.fa1, S.bsent, mask)
+    _send(g, topo, owner, T.lf[:, FW:256], T.asum[:, FW:256], S.fa1, S.fsent, mask)
     g.wait_ge(S.hf2, 1)
-    _send(g, topo, owner, T.lf[:, 0:FW], T.asum[:, 0:FW], S.fa2, S.bsent, mask)
-    g.wait_ge(S.bsent, 2 * n)
+    _send(g, topo, owner, T.lf[:, 0:FW], T.asum[:, 0:FW], S.fa2, S.fsent, mask)
+    g.wait_ge(S.bsent, len(_bits(xmask)))
+    g.wait_ge(S.fsent, 2 * len(_bits(mask)))
+
+
+def _weights(g, core, s, crew, T, topo):
+    S = T.sem
+    peers = [T.cores[(s + k) % N] for k in range(1, N)]
+    part = [q for q in "abcp" if crew["w" + q] == core][0]
+    view = _wview(T, s, part)
+    g.wait_ge(S.wr, len(_onchip(T.cores[s], core, peers[0], topo)))
+    if part in "ap":
+        mask = topo.mask(core, peers[0])
+        _spread(g, topo, peers, view, S["wa_%d" % s], S.bsent, mask)
+        g.wait_ge(S.bsent, len(_bits(mask)))
+        return
+    total = 0
+    for k in range(1, N):
+        f = _forwarder((s + k) % N, s, T, topo)
+        _send(g, topo, f, view, view, S["w" + part], S.bsent, topo.mask(core, f))
+        total += _count(core, f, topo)
+    g.wait_ge(S.bsent, total)
+
+
+def _forward(g, core, d, T, topo):
+    S = T.sem
+    owner = T.cores[d]
+    s = [k for k in range(N) if k != d and _forwarder(d, k, T, topo) == core][0]
+    crew = _crew(T.cores[s], topo)
+    for part, sem in (("b", "wa_%d"), ("c", "wb_%d")):
+        view = _wview(T, s, part)
+        g.wait_ge(S["w" + part], _count(crew["w" + part], core, topo))
+        _send(g, topo, owner, view, view, S[sem % s], S.bsent, topo.mask(core, owner))
+    g.wait_ge(S.bsent, 2 * _count(core, owner, topo))
 
 
 def _rank(g, core, r, T, topo):
@@ -142,19 +199,21 @@ def _rank(g, core, r, T, topo):
     Relu, Copy = ActivationFunctionType.Relu, ActivationFunctionType.Copy
     add, mx, mul = AluOpType.add, AluOpType.max, AluOpType.mult
     peers = [T.cores[(r + k) % N] for k in range(1, N)]
-    _, ra, rb, rp = _crew(core, topo)
+    crew = _crew(core, topo)
     off = topo.mask(core, peers[0])
-    rest = _onchip(core, ra, peers[0], topo)
+    rest = _onchip(core, crew["passer"], peers[0], topo)
+    on = _mask(rest)
     who = [(r - k) % N for k in range(N)]
-    n = len(_bits(off))
+    n, m = len(_bits(off)), len(rest)
+    hand = _count(crew["adder"], core, topo)
 
     sy.dma_start(T.xin[:], T.x[:]).then_inc(S.ld_x, 16)
     sy.dma_start(T.w1in[:], T.w1[:]).then_inc(S.ld_w1, 16)
     sy.dma_start(T.w3in[:], T.w3[:]).then_inc(S.ld_w3, 16)
     sy.dma_start(T.w4in[:], T.w4[:]).then_inc(S.ld_w4, 16)
     sy.dma_start(T.w2in[:], T.w2[:]).then_inc(S.ld_w2, 16)
-    sy.wait_ge(S.psent, N * n)
-    for k in range(N):
+    sy.wait_ge(S.psent, 4 * n + m)
+    for k in (1, 2, 3, 4, 0):
         sy.wait_ge(S["tl_%d" % k], 4)
         sy.dma_start(T.t[who[k]], T.tt[:, 512 * k:512 * k + 512]).then_inc(S.st, 16)
     sy.wait_ge(S.tlh, 4)
@@ -165,37 +224,36 @@ def _rank(g, core, r, T, topo):
 
     xs = T.xs[:, 128 * r:128 * r + 128]
     xq = T.xq[:, 128 * r:128 * r + 128].bitcast(dt.uint8)
+    xa = S["xa_%d" % r]
     g.wait_ge(S.q_x, 1)
-    _spread(g, topo, peers, xs, S["xa_%d" % r], S.bsent, off)
-    _spread(g, topo, peers[:2], xq, S["xa_%d" % r], S.bsent, off)
-    _spread(g, topo, peers[2:], xq, S["xa_%d" % r], S.bsent, off)
-    g.wait_ge(S.q_w34, 2)
-    half = len(rest) // 2
-    parts = []
-    for i, p in enumerate((ra, rb)):
-        a = WC * r + i * (WC // 2)
-        view = T.wq[:, a:a + WC // 2].bitcast(dt.uint8)
-        parts.append(RemoteDMATransfer(dst_ids=[_dst(p, topo)], dma_engine_mask=_mask(rest[half * i:half * i + half]),
-                                       remote_sem=S.wr, srcs=[view], dsts=[view]))
-    g.remote_dma_fused(parts, local_sem=S.bsent)
-    ws = T.ws[:, WC * r:WC * r + WC]
-    _send(g, topo, rp, ws, ws, S.wr, S.bsent, _mask(rest))
+    _send(g, topo, crew["passer"], xq, xq, S.xr, S.bsent, on)
+    for i, p in enumerate(peers[:ND]):
+        _send(g, topo, p, xs, xs, xa, S.bsent, off)
+        _send(g, topo, p, xq, xq, xa, S.bsent, off)
+        if i == 0:
+            _send(g, topo, crew["adder"], xs, xs, S.xr, S.bsent, on)
+    g.wait_ge(S.q_w3, 1)
+    for part in "bpac":
+        if part == "p":
+            g.wait_ge(S.q_w4, 1)
+        view = _wview(T, r, part)
+        _send(g, topo, crew["w" + part], view, view, S.wr, S.bsent, on)
     for k in range(1, N):
         owner = T.cores[who[k]]
-        adder = _crew(owner, topo)[0]
+        adder = _crew(owner, topo)["adder"]
         p = 256 * k
         g.wait_ge(S["ev_%d" % k], 2)
         if k < 3:
             _send(g, topo, adder, T.al[:, 256 * (k - 1):256 * k], T.pp[:, p:p + 256], S["ha%d" % k], S.psent, off)
         elif k == 3:
             _send(g, topo, adder, T.al[:, 512:512 + FW], T.pp[:, p:p + FW], S.ha3, S.psent, off)
-            _send(g, topo, owner, T.lc[:], T.pp[:, p + FW:p + 256], S.dc, S.psent, off)
+            _send(g, topo, crew["passer"], T.pb[:], T.pp[:, p + FW:p + 256], S.pr, S.psent, on)
         else:
             _send(g, topo, owner, T.ld[:], T.pp[:, p:p + 256], S.da, S.psent, off)
-    g.wait_ge(S.bsent, 3 * n + 2 * len(rest))
+    g.wait_ge(S.bsent, 2 * ND * n + 6 * m)
 
-    def bank(b):
-        return T.ps[:, 512 * b:512 * b + 128]
+    def bank(b, lo=0, hi=128):
+        return T.ps[:, 512 * b + lo:512 * b + hi]
 
     def act_v(buf, o, b, src, c, sem):
         v.tensor_scalar(buf[:, o + b:o + 512:4], src, 0.0, c, op0=mx, op1=mul).then_inc(sem, 1)
@@ -206,9 +264,9 @@ def _rank(g, core, r, T, topo):
         sc.activation(buf[:, o + b + 1:o + 512:4], src, Relu, scale=-c).then_inc(sem, 1)
 
     def zb(k): return 2 * (k % 2)
-    def sb(k): return 4 + 2 * (k % 2)
+    def sb(k): return 4 if k in (2, 4) else 6
     def vb(k): return 2 * (k % 3)
-    YB = 6
+    OWN, YB = 6, 6
 
     def t_z(k):
         s = who[k]
@@ -216,17 +274,16 @@ def _rank(g, core, r, T, topo):
             te.wait_ge(S["xa_%d" % s], 2 * n)
         else:
             te.wait_ge(S.q_x, 1)
-            te.wait_ge(S.q_w1, 1)
         for i in range(2):
             te.matmul_mx(bank(zb(k) + i), T.w1q[:, 128 * i:128 * i + 128], T.w1s[:, 128 * i:128 * i + 128],
                          T.xq[:, 128 * s:128 * s + 128], T.xs[:, 128 * s:128 * s + 128], True, True
                          ).then_inc(S["z%d_%d" % (i, k)], 1)
 
     def t_s(k):
-        if k == 0:
+        if k == 1:
             te.wait_ge(S.q_w2, 1)
-        if k >= 2:
-            te.wait_ge(S["ev_%d" % (k - 2)], 2)
+        if k in (0, 3, 4):
+            te.wait_ge(S["ev_%d" % (k - 2 if k else 3)], 2)
         te.wait_ge(S["qt_%d" % k], 1)
         for i in range(2):
             te.matmul_mx(bank(sb(k) + i), T.w2q[:, 128 * i:128 * i + 128], T.w2s[:, 128 * i:128 * i + 128],
@@ -238,26 +295,36 @@ def _rank(g, core, r, T, topo):
         if k:
             te.wait_ge(S["wa_%d" % s], 3 * n)
         else:
-            te.wait_ge(S.q_w34, 2)
-            te.wait_ge(S.ev_3, 2)
-            te.wait_ge(S.ev_4, 2)
+            te.wait_ge(S.q_w3, 1)
+            te.wait_ge(S.q_w4, 1)
+            te.wait_ge(S["ev_%d" % (N - 1)], 2)
             te.wait_ge(S.qh, 1)
+        if k > 2:
+            if k - 3 in BYS:
+                te.wait_ge(S["vh_%d" % (k - 3)], 1)
+            te.wait_ge(S["tu_%d" % (k - 3)], 3 if k - 3 in BYS else 4)
         for i in range(2):
             a = WC * s + 128 * i
             te.matmul_mx(bank(vb(k) + i), T.wq[:, a:a + 128], T.ws[:, a:a + 128], T.hq[:], T.hs[:], True, True
                          ).then_inc(S["v%d_%d" % (i, k)], 1)
 
     def t_y(k):
-        a = WC * who[k] + 256
+        s = who[k]
+        a = WC * s + 256
+        if k:
+            te.wait_ge(S["wb_%d" % s], n)
         te.wait_ge(S["qu_%d" % k], 1)
-        m = te.matmul_mx(bank(YB), T.wq[:, a:a + 128], T.ws[:, a:a + 128], T.uq[:, 128 * k:128 * k + 128],
+        o = te.matmul_mx(bank(YB), T.wq[:, a:a + 128], T.ws[:, a:a + 128], T.uq[:, 128 * k:128 * k + 128],
                          T.us[:, 128 * k:128 * k + 128], k == 0, k == N - 1)
         if k == N - 1:
-            m.then_inc(S.yd, 1)
+            o.then_inc(S.yd, 1)
 
-    t_z(0); t_s(0)
-    t_z(1); t_z(2); t_s(1); t_z(3); t_s(2); t_z(4); t_s(3); t_s(4)
-    t_v(0); t_v(1); t_v(2); t_y(0); t_v(3); t_y(1); t_v(4); t_y(2); t_y(3); t_y(4)
+    te.wait_ge(S.q_w1, 1)
+    t_z(1); t_z(2); t_s(1); t_z(3); t_s(2); t_z(4); t_s(3); t_s(4); t_z(0); t_s(0)
+    for k in range(N):
+        t_v(k)
+    for k in range(N):
+        t_y(k)
 
     def v_r(k):
         v.wait_ge(S["z0_%d" % k], 1)
@@ -274,10 +341,16 @@ def _rank(g, core, r, T, topo):
 
     def v_ru(k):
         v.wait_ge(S["v0_%d" % k], 1)
-        act_v(T.uu, 512 * k, 0, bank(vb(k)), C1, S["tu_%d" % k])
+        o = 512 * k
+        if k in BYS:
+            v.tensor_scalar(T.uu[:, o:o + 512:4], bank(vb(k)), 0.0, C1, op0=mx, op1=mul).then_inc(S["vh_%d" % k], 1)
+        else:
+            act_v(T.uu, o, 0, bank(vb(k)), C1, S["tu_%d" % k])
 
     def v_qu(k):
-        v.wait_ge(S["tu_%d" % k], 4)
+        if k in BYS:
+            v.wait_ge(S["vh_%d" % k], 1)
+        v.wait_ge(S["tu_%d" % k], 3 if k in BYS else 4)
         v.quantize_mx(T.uq[:, 128 * k:128 * k + 128], T.us[:, 128 * k:128 * k + 128], T.uu[:, 512 * k:512 * k + 512]
                       ).then_inc(S["qu_%d" % k], 1)
 
@@ -286,33 +359,30 @@ def _rank(g, core, r, T, topo):
     v.wait_ge(S.ld_w1, 16)
     v.quantize_mx(T.w1q[:], T.w1s[:], T.w1in[:]).then_inc(S.q_w1, 1)
     v.wait_ge(S.ld_w3, 16)
-    v.quantize_mx(T.wq[:, WC * r:WC * r + 256], T.ws[:, WC * r:WC * r + 256], T.w3in[:]).then_inc(S.q_w34, 1)
+    v.quantize_mx(T.wq[:, WC * r:WC * r + 256], T.ws[:, WC * r:WC * r + 256], T.w3in[:]).then_inc(S.q_w3, 1)
     v.wait_ge(S.ld_w4, 16)
-    v.quantize_mx(T.wq[:, WC * r + 256:WC * r + 384], T.ws[:, WC * r + 256:WC * r + 384], T.w4in[:]).then_inc(S.q_w34, 1)
-    v_r(0); v_q(0)
+    v.quantize_mx(T.wq[:, WC * r + 256:WC * r + 384], T.ws[:, WC * r + 256:WC * r + 384], T.w4in[:]).then_inc(S.q_w4, 1)
     v.wait_ge(S.ld_w2, 16)
     v.quantize_mx(T.w2q[:], T.w2s[:], T.w2in[:]).then_inc(S.q_w2, 1)
-    v_e(0)
-    v_r(1); v_q(1); v_r(2); v_e(1); v_q(2); v_r(3); v_e(2); v_q(3); v_r(4); v_e(3); v_q(4); v_e(4)
+    v_r(1); v_q(1); v_r(2); v_e(1); v_q(2); v_r(3); v_e(2); v_q(3); v_r(4); v_e(3); v_q(4); v_e(4); v_r(0); v_q(0)
 
-    def acc(a, b, src, sem):
-        v.tensor_tensor(T.pp[:, a:b], T.pp[:, a:b], src, add).then_inc(sem, 1)
-
-    v.wait_ge(S.ev_0, 2)
-    v.wait_ge(S.fa1, n)
-    acc(FW, 256, T.lf[:, FW:256], S.c1)
+    P = T.pp
+    v.wait_ge(S.s0_0, 1)
+    v.wait_ge(S.s1_0, 1)
+    v.wait_ge(S.fa1, hand)
+    v.tensor_tensor(P[:, FW:256], bank(OWN + 1, FW - 128), T.lf[:, FW:256], add).then_inc(S.c1, 1)
     v.wait_ge(S.c1, 1)
     v.wait_ge(S.dc, n)
-    acc(FW, 256, T.lc[:], S.c2)
-    v.wait_ge(S.c2, 1)
+    v.tensor_tensor(P[:, FW:256], P[:, FW:256], T.lc[:], add).then_inc(S.c2, 1)
+    v.wait_ge(S.fa2, hand)
+    v.tensor_tensor(P[:, 0:128], bank(OWN), T.lf[:, 0:128], add).then_inc(S.c2, 1)
+    v.tensor_tensor(P[:, 128:FW], bank(OWN + 1, 0, FW - 128), T.lf[:, 128:FW], add).then_inc(S.c2, 1)
+    v.wait_ge(S.c2, 3)
     v.wait_ge(S.da, n)
-    acc(0, 256, T.ld[:], S.c3)
-    v.wait_ge(S.c3, 1)
-    v.wait_ge(S.fa2, n)
-    acc(0, 128, T.lf[:, 0:128], S.hA)
-    acc(128, FW, T.lf[:, 128:FW], S.hB)
+    v.tensor_tensor(P[:, 0:128], P[:, 0:128], T.ld[:, 0:128], add).then_inc(S.hA, 1)
+    v.tensor_tensor(P[:, 128:256], P[:, 128:256], T.ld[:, 128:256], add).then_inc(S.hB, 1)
     v.wait_ge(S.hB, 1)
-    act_v(T.hh, 0, 2, T.pp[:, 128:256], C2, S.tlh)
+    v.tensor_scalar(T.hh[:, 2:512:4], P[:, 128:256], 0.0, C2, op0=mx, op1=mul).then_inc(S.tlh, 1)
     v.wait_ge(S.tlh, 4)
     v.quantize_mx(T.hq[:], T.hs[:], T.hh[:]).then_inc(S.qh, 1)
     v_ru(0); v_ru(1); v_qu(0); v_ru(2); v_qu(1); v_ru(3); v_qu(2); v_ru(4); v_qu(3); v_qu(4)
@@ -327,10 +397,14 @@ def _rank(g, core, r, T, topo):
         sc.wait_ge(S["s1_%d" % k], 1)
         sc.activation(T.pp[:, 256 * k + 128:256 * k + 256], bank(sb(k) + 1), Copy).then_inc(S["ev_%d" % k], 1)
 
-    s_r(0); s_e(0)
-    s_r(1); s_r(2); s_e(1); s_r(3); s_e(2); s_r(4); s_e(3); s_e(4)
+    s_r(1); s_r(2); s_e(1); s_r(3); s_e(2); s_r(4); s_e(3); s_e(4); s_r(0)
     sc.wait_ge(S.hA, 1)
-    act_s(T.hh, 0, 0, T.pp[:, 0:128], C2, S.tlh)
+    act_s(T.hh, 0, 0, P[:, 0:128], C2, S.tlh)
+    sc.wait_ge(S.hB, 1)
+    sc.activation(T.hh[:, 3:512:4], P[:, 128:256], Relu, scale=-C2).then_inc(S.tlh, 1)
     for k in range(N):
         sc.wait_ge(S["v1_%d" % k], 1)
         act_s(T.uu, 512 * k, 2, bank(vb(k) + 1), C1, S["tu_%d" % k])
+        if k in BYS:
+            sc.wait_ge(S["vh_%d" % k], 1)
+            sc.activation(T.uu[:, 512 * k + 1:512 * k + 512:4], bank(vb(k)), Relu, scale=-C1).then_inc(S["tu_%d" % k], 1)

import numpy as np
from concourse.bass import DstId, RemoteDMATransfer
from concourse.mybir import dt, AluOpType, ActivationFunctionType

N = 5
SIM_CORES = 96
C1 = float(np.float32(0.041))
C2 = float(np.float32(0.01834))
FW = 160
WC = 384
ND = 3
BYS = (1, 3)

CODES = "float8_e4m3fn_x4"
SCRATCH = {
    "xin": ("sbuf", [128, 512], "bfloat16"),
    "w1in": ("sbuf", [128, 1024], "bfloat16"),
    "w2in": ("sbuf", [128, 1024], "bfloat16"),
    "w3in": ("sbuf", [128, 1024], "bfloat16"),
    "w4in": ("sbuf", [128, 512], "bfloat16"),
    "xq": ("sbuf", [128, N * 128], CODES),
    "xs": ("sbuf", [128, N * 128], "uint8"),
    "w1q": ("sbuf", [128, 256], CODES),
    "w1s": ("sbuf", [128, 256], "uint8"),
    "w2q": ("sbuf", [128, 256], CODES),
    "w2s": ("sbuf", [128, 256], "uint8"),
    "wq": ("sbuf", [128, N * WC], CODES),
    "ws": ("sbuf", [128, N * WC], "uint8"),
    "tt": ("sbuf", [128, N * 512], "bfloat16"),
    "tq": ("sbuf", [128, N * 128], CODES),
    "ts": ("sbuf", [128, N * 128], "uint8"),
    "hh": ("sbuf", [128, 512], "bfloat16"),
    "hq": ("sbuf", [128, 128], CODES),
    "hs": ("sbuf", [128, 128], "uint8"),
    "uu": ("sbuf", [128, N * 512], "bfloat16"),
    "uq": ("sbuf", [128, N * 128], CODES),
    "us": ("sbuf", [128, N * 128], "uint8"),
    "pp": ("sbuf", [128, N * 256], "float32"),
    "ld": ("sbuf", [128, 256], "float32"),
    "lc": ("sbuf", [128, 256 - FW], "float32"),
    "pb": ("sbuf", [128, 256 - FW], "float32"),
    "lf": ("sbuf", [128, 256], "float32"),
    "al": ("sbuf", [128, 768], "float32"),
    "asum": ("sbuf", [128, 256], "float32"),
    "yo": ("sbuf", [128, 128], "float32"),
    "ps": ("psum", [128, 4096], "float32"),
}
_ONE = ["ld_x", "ld_w1", "ld_w2", "ld_w3", "ld_w4", "q_x", "q_w1", "q_w2", "q_w3", "q_w4", "c1", "c2", "hA", "hB", "tlh", "qh",
        "yd", "yev", "st", "bsent", "psent", "fsent", "da", "dc", "fa1", "fa2", "ha1", "ha2", "ha3", "hb", "hf1", "hf2",
        "wr", "wb", "wc", "xr", "pr"]
_FIVE = ["z0_", "z1_", "tl_", "qt_", "s0_", "s1_", "ev_", "v0_", "v1_", "vh_", "tu_", "qu_", "xa_", "wa_", "wb_"]
SEMAPHORES = _ONE + [n + str(k) for n in _FIVE for k in range(N)]


def _bits(mask):
    return [b for b in range(mask.bit_length()) if (mask >> b) & 1]


def _mask(bits):
    m = 0
    for b in bits:
        m |= 1 << b
    return m


def _count(src, dst, topo):
    return len(_bits(topo.mask(src, dst)))


def _crew(c, topo):
    mate = [k for k in range(SIM_CORES) if topo.mates(topo.chip(k), topo.chip(c))]
    chip = sorted((k for k in range(SIM_CORES) if k != c and topo.chip(k) == topo.chip(c)),
                  key=lambda k: topo.may_write(k, mate[0]))
    near = [k for k in chip if topo.die(k) == topo.die(c)]
    far = [k for k in chip if topo.die(k) != topo.die(c)]
    return {"adder": near[0], "passer": near[1], "wb": near[2], "wa": far[0], "wp": far[1], "wc": far[-1],
            "fw": [k for k in mate if topo.may_write(k, c)]}


def _forwarder(d, s, T, topo):
    return _crew(T.cores[d], topo)["fw"][(d - s) % N - 1]


def _onchip(c, near, far, topo):
    return _bits(topo.mask(c, near) & ~topo.mask(c, far))


def _dst(c, topo):
    rid, pid, _ = topo.addr(c)
    return DstId(rid=rid, pnc=pid)


def _send(g, topo, dst, out, in_, sem, lsem, mask):
    rid, pid, _ = topo.addr(dst)
    g.remote_dma(out_ap=out, in_ap=in_, remote_sem=sem, local_sem=lsem, pid=pid, routing_id=rid, dma_engine_mask=mask)


def _spread(g, topo, dsts, view, sem, lsem, mask):
    g.remote_dma_fused([RemoteDMATransfer(dst_ids=[_dst(p, topo) for p in dsts], dma_engine_mask=mask, remote_sem=sem,
                                          srcs=[view], dsts=[view for p in dsts])], local_sem=lsem)


def _wview(T, s, part):
    if part == "p":
        return T.ws[:, WC * s:WC * s + WC]
    a = WC * s + 128 * "abc".index(part)
    return T.wq[:, a:a + 128].bitcast(dt.uint8)


def rank_program(g, core, T, topo):
    rank = T.rank_of(core)
    if rank is not None:
        _rank(g, core, rank, T, topo)
        return
    for s in range(N):
        crew = _crew(T.cores[s], topo)
        if core == crew["adder"]:
            _adder(g, core, s, T, topo)
        elif core == crew["passer"]:
            _passer(g, core, s, T, topo)
        elif core in (crew["wa"], crew["wb"], crew["wc"], crew["wp"]):
            _weights(g, core, s, crew, T, topo)
        elif core in crew["fw"]:
            _forward(g, core, s, T, topo)


def _relay_x(g, core, s, view, T, topo):
    S = T.sem
    peers = [T.cores[(s + k) % N] for k in range(1 + ND, N)]
    mask = topo.mask(core, peers[0])
    g.wait_ge(S.xr, len(_onchip(T.cores[s], core, peers[0], topo)))
    _spread(g, topo, peers, view, S["xa_%d" % s], S.bsent, mask)
    return mask


def _passer(g, core, s, T, topo):
    S = T.sem
    mask = _relay_x(g, core, s, T.xq[:, 128 * s:128 * s + 128].bitcast(dt.uint8), T, topo)
    owner = T.cores[(s - 3) % N]
    g.wait_ge(S.pr, len(_onchip(T.cores[s], core, owner, topo)))
    _send(g, topo, owner, T.lc[:], T.pb[:], S.dc, S.bsent, mask)
    g.wait_ge(S.bsent, 2 * len(_bits(mask)))


def _adder(g, core, s, T, topo):
    S, v = T.sem, g.vector
    owner, far = T.cores[s], T.cores[(s + 1) % N]
    mask = topo.mask(core, owner)
    came = _count(far, core, topo)
    v.wait_ge(S.ha1, came)
    v.wait_ge(S.ha2, came)
    v.tensor_tensor(T.asum[:, FW:256], T.al[:, FW:256], T.al[:, 256 + FW:512], AluOpType.add).then_inc(S.hf1, 1)
    v.tensor_tensor(T.asum[:, 0:FW], T.al[:, 0:FW], T.al[:, 256:256 + FW], AluOpType.add).then_inc(S.hb, 1)
    v.wait_ge(S.hb, 1)
    v.wait_ge(S.ha3, came)
    v.tensor_tensor(T.asum[:, 0:FW], T.asum[:, 0:FW], T.al[:, 512:512 + FW], AluOpType.add).then_inc(S.hf2, 1)
    xmask = _relay_x(g, core, s, T.xs[:, 128 * s:128 * s + 128], T, topo)
    g.wait_ge(S.hf1, 1)
    _send(g, topo, owner, T.lf[:, FW:256], T.asum[:, FW:256], S.fa1, S.fsent, mask)
    g.wait_ge(S.hf2, 1)
    _send(g, topo, owner, T.lf[:, 0:FW], T.asum[:, 0:FW], S.fa2, S.fsent, mask)
    g.wait_ge(S.bsent, len(_bits(xmask)))
    g.wait_ge(S.fsent, 2 * len(_bits(mask)))


def _weights(g, core, s, crew, T, topo):
    S = T.sem
    peers = [T.cores[(s + k) % N] for k in range(1, N)]
    part = [q for q in "abcp" if crew["w" + q] == core][0]
    view = _wview(T, s, part)
    g.wait_ge(S.wr, len(_onchip(T.cores[s], core, peers[0], topo)))
    if part in "ap":
        mask = topo.mask(core, peers[0])
        _spread(g, topo, peers, view, S["wa_%d" % s], S.bsent, mask)
        g.wait_ge(S.bsent, len(_bits(mask)))
        return
    total = 0
    for k in range(1, N):
        f = _forwarder((s + k) % N, s, T, topo)
        _send(g, topo, f, view, view, S["w" + part], S.bsent, topo.mask(core, f))
        total += _count(core, f, topo)
    g.wait_ge(S.bsent, total)


def _forward(g, core, d, T, topo):
    S = T.sem
    owner = T.cores[d]
    s = [k for k in range(N) if k != d and _forwarder(d, k, T, topo) == core][0]
    crew = _crew(T.cores[s], topo)
    for part, sem in (("b", "wa_%d"), ("c", "wb_%d")):
        view = _wview(T, s, part)
        g.wait_ge(S["w" + part], _count(crew["w" + part], core, topo))
        _send(g, topo, owner, view, view, S[sem % s], S.bsent, topo.mask(core, owner))
    g.wait_ge(S.bsent, 2 * _count(core, owner, topo))


def _rank(g, core, r, T, topo):
    S, v, sc, te, sy = T.sem, g.vector, g.scalar, g.tensor, g.sync
    Relu, Copy = ActivationFunctionType.Relu, ActivationFunctionType.Copy
    add, mx, mul = AluOpType.add, AluOpType.max, AluOpType.mult
    peers = [T.cores[(r + k) % N] for k in range(1, N)]
    crew = _crew(core, topo)
    off = topo.mask(core, peers[0])
    rest = _onchip(core, crew["passer"], peers[0], topo)
    on = _mask(rest)
    who = [(r - k) % N for k in range(N)]
    n, m = len(_bits(off)), len(rest)
    hand = _count(crew["adder"], core, topo)

    sy.dma_start(T.xin[:], T.x[:]).then_inc(S.ld_x, 16)
    sy.dma_start(T.w1in[:], T.w1[:]).then_inc(S.ld_w1, 16)
    sy.dma_start(T.w3in[:], T.w3[:]).then_inc(S.ld_w3, 16)
    sy.dma_start(T.w4in[:], T.w4[:]).then_inc(S.ld_w4, 16)
    sy.dma_start(T.w2in[:], T.w2[:]).then_inc(S.ld_w2, 16)
    sy.wait_ge(S.psent, 4 * n + m)
    for k in (1, 2, 3, 4, 0):
        sy.wait_ge(S["tl_%d" % k], 4)
        sy.dma_start(T.t[who[k]], T.tt[:, 512 * k:512 * k + 512]).then_inc(S.st, 16)
    sy.wait_ge(S.tlh, 4)
    sy.dma_start(T.h[:], T.hh[:]).then_inc(S.st, 16)
    sy.wait_ge(S.yev, 1)
    sy.dma_start(T.y[:], T.yo[:]).then_inc(S.st, 16)
    sy.wait_ge(S.st, 16 * (N + 2))

    xs = T.xs[:, 128 * r:128 * r + 128]
    xq = T.xq[:, 128 * r:128 * r + 128].bitcast(dt.uint8)
    xa = S["xa_%d" % r]
    g.wait_ge(S.q_x, 1)
    _send(g, topo, crew["passer"], xq, xq, S.xr, S.bsent, on)
    for i, p in enumerate(peers[:ND]):
        _send(g, topo, p, xs, xs, xa, S.bsent, off)
        _send(g, topo, p, xq, xq, xa, S.bsent, off)
        if i == 0:
            _send(g, topo, crew["adder"], xs, xs, S.xr, S.bsent, on)
    g.wait_ge(S.q_w3, 1)
    for part in "bpac":
        if part == "p":
            g.wait_ge(S.q_w4, 1)
        view = _wview(T, r, part)
        _send(g, topo, crew["w" + part], view, view, S.wr, S.bsent, on)
    for k in range(1, N):
        owner = T.cores[who[k]]
        adder = _crew(owner, topo)["adder"]
        p = 256 * k
        g.wait_ge(S["ev_%d" % k], 2)
        if k < 3:
            _send(g, topo, adder, T.al[:, 256 * (k - 1):256 * k], T.pp[:, p:p + 256], S["ha%d" % k], S.psent, off)
        elif k == 3:
            _send(g, topo, adder, T.al[:, 512:512 + FW], T.pp[:, p:p + FW], S.ha3, S.psent, off)
            _send(g, topo, crew["passer"], T.pb[:], T.pp[:, p + FW:p + 256], S.pr, S.psent, on)
        else:
            _send(g, topo, owner, T.ld[:], T.pp[:, p:p + 256], S.da, S.psent, off)
    g.wait_ge(S.bsent, 2 * ND * n + 6 * m)

    def bank(b, lo=0, hi=128):
        return T.ps[:, 512 * b + lo:512 * b + hi]

    def act_v(buf, o, b, src, c, sem):
        v.tensor_scalar(buf[:, o + b:o + 512:4], src, 0.0, c, op0=mx, op1=mul).then_inc(sem, 1)
        v.tensor_scalar(buf[:, o + b + 1:o + 512:4], src, -c, 0.0, op0=mul, op1=mx).then_inc(sem, 1)

    def act_s(buf, o, b, src, c, sem):
        sc.activation(buf[:, o + b:o + 512:4], src, Relu, scale=c).then_inc(sem, 1)
        sc.activation(buf[:, o + b + 1:o + 512:4], src, Relu, scale=-c).then_inc(sem, 1)

    def zb(k): return 2 * (k % 2)
    def sb(k): return 4 if k in (2, 4) else 6
    def vb(k): return 2 * (k % 3)
    OWN, YB = 6, 6

    def t_z(k):
        s = who[k]
        if k:
            te.wait_ge(S["xa_%d" % s], 2 * n)
        else:
            te.wait_ge(S.q_x, 1)
        for i in range(2):
            te.matmul_mx(bank(zb(k) + i), T.w1q[:, 128 * i:128 * i + 128], T.w1s[:, 128 * i:128 * i + 128],
                         T.xq[:, 128 * s:128 * s + 128], T.xs[:, 128 * s:128 * s + 128], True, True
                         ).then_inc(S["z%d_%d" % (i, k)], 1)

    def t_s(k):
        if k == 1:
            te.wait_ge(S.q_w2, 1)
        if k in (0, 3, 4):
            te.wait_ge(S["ev_%d" % (k - 2 if k else 3)], 2)
        te.wait_ge(S["qt_%d" % k], 1)
        for i in range(2):
            te.matmul_mx(bank(sb(k) + i), T.w2q[:, 128 * i:128 * i + 128], T.w2s[:, 128 * i:128 * i + 128],
                         T.tq[:, 128 * k:128 * k + 128], T.ts[:, 128 * k:128 * k + 128], True, True
                         ).then_inc(S["s%d_%d" % (i, k)], 1)

    def t_v(k):
        s = who[k]
        if k:
            te.wait_ge(S["wa_%d" % s], 3 * n)
        else:
            te.wait_ge(S.q_w3, 1)
            te.wait_ge(S.q_w4, 1)
            te.wait_ge(S["ev_%d" % (N - 1)], 2)
            te.wait_ge(S.qh, 1)
        if k > 2:
            if k - 3 in BYS:
                te.wait_ge(S["vh_%d" % (k - 3)], 1)
            te.wait_ge(S["tu_%d" % (k - 3)], 3 if k - 3 in BYS else 4)
        for i in range(2):
            a = WC * s + 128 * i
            te.matmul_mx(bank(vb(k) + i), T.wq[:, a:a + 128], T.ws[:, a:a + 128], T.hq[:], T.hs[:], True, True
                         ).then_inc(S["v%d_%d" % (i, k)], 1)

    def t_y(k):
        s = who[k]
        a = WC * s + 256
        if k:
            te.wait_ge(S["wb_%d" % s], n)
        te.wait_ge(S["qu_%d" % k], 1)
        o = te.matmul_mx(bank(YB), T.wq[:, a:a + 128], T.ws[:, a:a + 128], T.uq[:, 128 * k:128 * k + 128],
                         T.us[:, 128 * k:128 * k + 128], k == 0, k == N - 1)
        if k == N - 1:
            o.then_inc(S.yd, 1)

    te.wait_ge(S.q_w1, 1)
    t_z(1); t_z(2); t_s(1); t_z(3); t_s(2); t_z(4); t_s(3); t_s(4); t_z(0); t_s(0)
    for k in range(N):
        t_v(k)
    for k in range(N):
        t_y(k)

    def v_r(k):
        v.wait_ge(S["z0_%d" % k], 1)
        act_v(T.tt, 512 * k, 0, bank(zb(k)), C1, S["tl_%d" % k])

    def v_q(k):
        v.wait_ge(S["tl_%d" % k], 4)
        v.quantize_mx(T.tq[:, 128 * k:128 * k + 128], T.ts[:, 128 * k:128 * k + 128], T.tt[:, 512 * k:512 * k + 512]
                      ).then_inc(S["qt_%d" % k], 1)

    def v_e(k):
        v.wait_ge(S["s0_%d" % k], 1)
        v.tensor_copy(T.pp[:, 256 * k:256 * k + 128], bank(sb(k))).then_inc(S["ev_%d" % k], 1)

    def v_ru(k):
        v.wait_ge(S["v0_%d" % k], 1)
        o = 512 * k
        if k in BYS:
            v.tensor_scalar(T.uu[:, o:o + 512:4], bank(vb(k)), 0.0, C1, op0=mx, op1=mul).then_inc(S["vh_%d" % k], 1)
        else:
            act_v(T.uu, o, 0, bank(vb(k)), C1, S["tu_%d" % k])

    def v_qu(k):
        if k in BYS:
            v.wait_ge(S["vh_%d" % k], 1)
        v.wait_ge(S["tu_%d" % k], 3 if k in BYS else 4)
        v.quantize_mx(T.uq[:, 128 * k:128 * k + 128], T.us[:, 128 * k:128 * k + 128], T.uu[:, 512 * k:512 * k + 512]
                      ).then_inc(S["qu_%d" % k], 1)

    v.wait_ge(S.ld_x, 16)
    v.quantize_mx(T.xq[:, 128 * r:128 * r + 128], T.xs[:, 128 * r:128 * r + 128], T.xin[:]).then_inc(S.q_x, 1)
    v.wait_ge(S.ld_w1, 16)
    v.quantize_mx(T.w1q[:], T.w1s[:], T.w1in[:]).then_inc(S.q_w1, 1)
    v.wait_ge(S.ld_w3, 16)
    v.quantize_mx(T.wq[:, WC * r:WC * r + 256], T.ws[:, WC * r:WC * r + 256], T.w3in[:]).then_inc(S.q_w3, 1)
    v.wait_ge(S.ld_w4, 16)
    v.quantize_mx(T.wq[:, WC * r + 256:WC * r + 384], T.ws[:, WC * r + 256:WC * r + 384], T.w4in[:]).then_inc(S.q_w4, 1)
    v.wait_ge(S.ld_w2, 16)
    v.quantize_mx(T.w2q[:], T.w2s[:], T.w2in[:]).then_inc(S.q_w2, 1)
    v_r(1); v_q(1); v_r(2); v_e(1); v_q(2); v_r(3); v_e(2); v_q(3); v_r(4); v_e(3); v_q(4); v_e(4); v_r(0); v_q(0)

    P = T.pp
    v.wait_ge(S.s0_0, 1)
    v.wait_ge(S.s1_0, 1)
    v.wait_ge(S.fa1, hand)
    v.tensor_tensor(P[:, FW:256], bank(OWN + 1, FW - 128), T.lf[:, FW:256], add).then_inc(S.c1, 1)
    v.wait_ge(S.c1, 1)
    v.wait_ge(S.dc, n)
    v.tensor_tensor(P[:, FW:256], P[:, FW:256], T.lc[:], add).then_inc(S.c2, 1)
    v.wait_ge(S.fa2, hand)
    v.tensor_tensor(P[:, 0:128], bank(OWN), T.lf[:, 0:128], add).then_inc(S.c2, 1)
    v.tensor_tensor(P[:, 128:FW], bank(OWN + 1, 0, FW - 128), T.lf[:, 128:FW], add).then_inc(S.c2, 1)
    v.wait_ge(S.c2, 3)
    v.wait_ge(S.da, n)
    v.tensor_tensor(P[:, 0:128], P[:, 0:128], T.ld[:, 0:128], add).then_inc(S.hA, 1)
    v.tensor_tensor(P[:, 128:256], P[:, 128:256], T.ld[:, 128:256], add).then_inc(S.hB, 1)
    v.wait_ge(S.hB, 1)
    v.tensor_scalar(T.hh[:, 2:512:4], P[:, 128:256], 0.0, C2, op0=mx, op1=mul).then_inc(S.tlh, 1)
    v.wait_ge(S.tlh, 4)
    v.quantize_mx(T.hq[:], T.hs[:], T.hh[:]).then_inc(S.qh, 1)
    v_ru(0); v_ru(1); v_qu(0); v_ru(2); v_qu(1); v_ru(3); v_qu(2); v_ru(4); v_qu(3); v_qu(4)
    v.wait_ge(S.yd, 1)
    v.tensor_copy(T.yo[:], bank(YB)).then_inc(S.yev, 1)

    def s_r(k):
        sc.wait_ge(S["z1_%d" % k], 1)
        act_s(T.tt, 512 * k, 2, bank(zb(k) + 1), C1, S["tl_%d" % k])

    def s_e(k):
        sc.wait_ge(S["s1_%d" % k], 1)
        sc.activation(T.pp[:, 256 * k + 128:256 * k + 256], bank(sb(k) + 1), Copy).then_inc(S["ev_%d" % k], 1)

    s_r(1); s_r(2); s_e(1); s_r(3); s_e(2); s_r(4); s_e(3); s_e(4); s_r(0)
    sc.wait_ge(S.hA, 1)
    act_s(T.hh, 0, 0, P[:, 0:128], C2, S.tlh)
    sc.wait_ge(S.hB, 1)
    sc.activation(T.hh[:, 3:512:4], P[:, 128:256], Relu, scale=-C2).then_inc(S.tlh, 1)
    for k in range(N):
        sc.wait_ge(S["v1_%d" % k], 1)
        act_s(T.uu, 512 * k, 2, bank(vb(k) + 1), C1, S["tu_%d" % k])
        if k in BYS:
            sc.wait_ge(S["vh_%d" % k], 1)
            sc.activation(T.uu[:, 512 * k + 1:512 * k + 512:4], bank(vb(k)), Relu, scale=-C1).then_inc(S["tu_%d" % k], 1)
